import numpy as np
import ml_dtypes


def mxq(x, axis, fmt="e4m3"):
    dtype, down = {"e4m3": (ml_dtypes.float8_e4m3fn, 7), "e5m2": (ml_dtypes.float8_e5m2, 14)}[fmt]
    v = np.moveaxis(np.asarray(x, np.float32).astype(ml_dtypes.bfloat16).astype(np.float64), axis, -1)
    blocks = v.reshape(v.shape[:-1] + (-1, 32))
    amax = np.abs(blocks).max(-1, keepdims=True)
    byte = np.maximum(np.where(amax > 0, np.frexp(amax)[1] - 1 + 127, 0) - down, 1)
    scale = np.exp2(byte - 127.0)
    codes = (blocks / scale).astype(np.float32).astype(dtype).astype(np.float64)
    return np.moveaxis((codes * scale).reshape(v.shape), -1, axis)


WIDE = False


def mx_kscale(k):
    if not WIDE:
        return np.ones(k)
    levels = np.array([10, -10, 5, -5, 0])
    if k % 512:
        return np.exp2(np.random.permutation(np.resize(levels, k // 32))).repeat(32)
    a = np.empty((k // 512, 16))
    for p in range(k // 512):
        a[p, :8] = np.random.permutation(np.resize(levels, 8))
        for g in range(8):
            far = levels[np.abs(levels - a[p, g]) >= 10]
            a[p, g + 8] = far[np.random.randint(len(far))]
    return np.exp2(a.ravel()).repeat(32)


def f64(x):
    return np.asarray(x).astype(np.float64)


def striped8(idx):
    return np.asarray(idx).reshape(8, -1, 16).transpose(0, 2, 1).reshape(128, -1).astype(np.uint16)


def unstriped8(offs):
    return offs.reshape(8, 16, -1).transpose(0, 2, 1).reshape(8, -1).astype(np.int64)


def pick8(x, idx, run):
    r = np.arange(len(x))
    return x[r[:, None], idx[r % (8 * run) // run]]


E2M1 = np.array([0.0, 0.5, 1.0, 1.5, 2.0, 3.0, 4.0, 6.0, -0.0, -0.5, -1.0, -1.5, -2.0, -3.0, -4.0, -6.0])


def pack_weight(w, fmt):
    k, n = w.shape
    w = f64(np.asarray(w, np.float32).astype(ml_dtypes.bfloat16)).reshape(k // 32, 32, n)
    amax = np.abs(w).max(1)
    if fmt == "e4m3":
        byte = np.frexp(amax)[1] - 1 + 127 - 7
    else:
        mant, ex = np.frexp(amax / 6.0)
        byte = np.where(mant > 0.5, ex, ex - 1) + 127
    byte = np.clip(np.where(amax > 0, byte, 1), 1, 254)
    scaled = (w * np.exp2(127.0 - byte)[:, None, :]).reshape(k, n).astype(np.float32)
    by_word = np.ascontiguousarray(scaled.reshape(k // 512, 128, 4, n).transpose(0, 1, 3, 2))
    if fmt == "e4m3":
        words = by_word.astype(ml_dtypes.float8_e4m3fn).view(np.uint8)
    else:
        c = by_word.astype(ml_dtypes.float4_e2m1fn).view(np.uint8) & 0xF
        words = (c[..., 0::2] | (c[..., 1::2] << 4)).reshape(k // 512, 128, 2 * n)
    return np.ascontiguousarray(words), np.ascontiguousarray(byte.astype(np.uint8).reshape(k // 512, 16, n))


def unpack_weight(words, scales, fmt):
    g, _, n = scales.shape
    words = np.ascontiguousarray(words).reshape(g, 128, n, -1)
    if fmt == "e4m3":
        vals = words.view(ml_dtypes.float8_e4m3fn).astype(np.float64)
    else:
        nib = np.empty((g, 128, n, 4), np.uint8)
        nib[..., 0::2] = words & 0xF
        nib[..., 1::2] = words >> 4
        vals = E2M1[nib]
    vals = vals * np.repeat(np.exp2(scales.astype(np.float64) - 127.0), 8, axis=1)[..., None]
    return vals.transpose(0, 1, 3, 2).reshape(g * 512, n)


D, V, Q, I = 512, 2048, 128, 512


def setup_inputs():
    n = np.random.standard_normal
    idx = np.stack([np.random.permutation(V)[:I] for _ in range(8)])
    fd = mx_kscale(D)
    vocp = pack_weight(n((D, V)) / fd[:, None], "e2m1")
    return {
        "hid": (n((D, Q)) * 0.7 / np.sqrt(D) * fd[:, None]).astype(np.float32),
        "voc_words": vocp[0],
        "voc_scales": vocp[1],
        "lpo": (np.random.uniform(-8.2, -7.2, (Q, I))).astype(np.float32),
        "adv": (1.0 * n((Q, I))).astype(np.float32),
        "old": (0.5 * n((Q, V))).astype(np.float32),
        "offs": striped8(idx),
    }


def reference(hid, voc_words, voc_scales, lpo, adv, old, offs):
    idx = unstriped8(offs)
    vocu = unpack_weight(voc_words, voc_scales, "e2m1")
    hidq = mxq(f64(hid), 0, "e4m3")
    a = hidq.T @ vocu
    p = np.exp(a)
    z = np.sum(p, axis=1, keepdims=True)
    r = np.exp(pick8(a, idx, 16) - np.log(z) - f64(lpo))
    dz = np.sum(f64(adv) * r * (-1.0), axis=1, keepdims=True) / z
    e1 = f64(adv) * r
    s1 = np.zeros((Q, V))
    s1[np.arange(Q)[:, None], idx[np.arange(Q) % 128 // 16]] = e1
    da = dz * p + s1
    y = da * 1.0 + f64(old)
    return y

@@ -1,0 +1,176 @@
+from contextlib import ExitStack
+
+import concourse.mybir as mybir
+from concourse.masks import make_identity
+
+D, V, Q, LISTED = 512, 2048, 128, 512
+FLOPS = 2 * D * V * Q
+
+F32 = mybir.dt.float32
+BF16 = mybir.dt.bfloat16
+I32 = mybir.dt.int32
+U32 = mybir.dt.uint32
+U16 = mybir.dt.uint16
+U8 = mybir.dt.uint8
+FP8X4 = mybir.dt.float8_e4m3fn_x4
+FP4X4 = mybir.dt.float4_e2m1fn_x4
+ALU = mybir.AluOpType
+ACT = mybir.ActivationFunctionType
+
+P = 128
+PACK = 4
+CHUNK = 512
+CHUNKS = V // CHUNK
+HALF = V // 2
+BLOCKS = CHUNK // P
+
+
+def tile_attend_bpolicyratio_heads_kernel(tc, hid, voc_words, voc_scales, lpo, adv, old, offs, out):
+    nc = tc.nc
+    with ExitStack() as ctx:
+        sb = ctx.enter_context(tc.tile_pool(name="sb", bufs=1))
+        ring = ctx.enter_context(tc.tile_pool(name="ring", bufs=2))
+        ps_row = ctx.enter_context(tc.psum_pool(name="ps_row", bufs=CHUNKS))
+        ps_col = ctx.enter_context(tc.psum_pool(name="ps_col", bufs=CHUNKS - 1))
+
+        offsets = sb.tile([P, LISTED // 16], U16, name="offsets")
+        voc_plane = sb.tile([P, V], U8, name="voc_plane", align_bytes=64)
+        nc.vector.memset(voc_plane[:].bitcast(I32), 0)
+        warm_in = sb.tile([P, 1], F32, name="warm_in")
+        nc.gpsimd.memset(warm_in[:], 0.0)
+        warm_out = sb.tile([P, 1], F32, name="warm_out")
+        nc.scalar.activation(warm_out[:], warm_in[:], ACT.Exp)
+
+        hid_raw = sb.tile([P, PACK, Q], F32, name="hid_raw")
+        nc.sync.dma_start(out=hid_raw[:], in_=hid.rearrange("(p t) q -> p t q", t=PACK))
+        for quad in range(4):
+            nc.sync.dma_start(
+                out=voc_plane[32 * quad : 32 * quad + 4, :].bitcast(I32),
+                in_=voc_scales[0, 4 * quad : 4 * quad + 4, :].bitcast(I32),
+            )
+        words = []
+        for half in range(2):
+            w = sb.tile([P, 2 * HALF], U8, name="words%d" % half, align_bytes=64)
+            nc.sync.dma_start(out=w[:].bitcast(I32), in_=voc_words[0, :, half * 2 * HALF : (half + 1) * 2 * HALF].bitcast(I32))
+            words.append(w)
+        nc.sync.dma_start(offsets[:], offs)
+        lpo_sb = sb.tile([P, LISTED], F32, name="lpo_sb")
+        nc.sync.dma_start(out=lpo_sb[:], in_=lpo)
+        adv_sb = sb.tile([P, LISTED], F32, name="adv_sb")
+        nc.sync.dma_start(out=adv_sb[:], in_=adv)
+        old_sb = []
+        for c in range(CHUNKS):
+            o = sb.tile([P, CHUNK], F32, name="old%d" % c)
+            nc.sync.dma_start(out=o[:], in_=old[:, c * CHUNK : (c + 1) * CHUNK])
+            old_sb.append(o)
+
+        placed = sb.tile([P, V], F32, name="placed")
+        nc.vector.memset(placed[:], 0.0)
+        ident = sb.tile([P, P], F32, name="ident")
+        make_identity(nc, ident[:])
+
+        hid_bf = sb.tile([P, Q, PACK], BF16, name="hid_bf", align_bytes=64)
+        nc.vector.tensor_copy(
+            out=hid_bf[:].rearrange("p (c i) t -> p c t i", i=4),
+            in_=hid_raw[:].rearrange("p t (c i) -> p c t i", i=4),
+        )
+        hid_codes = sb.tile([P, Q], U32, name="hid_codes", align_bytes=64)
+        hid_plane = sb.tile([P, Q], U8, name="hid_plane", align_bytes=64)
+        nc.vector.quantize_mx(out=hid_codes[:].bitcast(FP8X4), scales=hid_plane[:], in_=hid_bf[:].rearrange("p q t -> p (q t)"))
+
+        scores = sb.tile([P, V], F32, name="scores")
+        chunk_max = sb.tile([P, CHUNKS], F32, name="chunk_max")
+        chunk_sum = sb.tile([P, CHUNKS], F32, name="chunk_sum")
+        probs = []
+        for c in range(CHUNKS):
+            cols = slice(c * CHUNK, (c + 1) * CHUNK)
+            bank = ps_row.tile([P, CHUNK], F32, name="bank", tag="row")
+            nc.tensor.matmul_mx(
+                out=bank[:],
+                lhsT=hid_codes[:].bitcast(FP8X4),
+                lhsT_scale=hid_plane[:],
+                rhs=words[c // 2][:, (c % 2) * 2 * CHUNK : (c % 2 + 1) * 2 * CHUNK].bitcast(FP4X4),
+                rhs_scale=voc_plane[:, cols],
+                start=True,
+                stop=True,
+            )
+            nc.vector.tensor_scalar(
+                out=scores[:, cols], in0=bank[:], scalar1=1.0, scalar2=None,
+                op0=ALU.mult, op1=ALU.max, accum_out=chunk_max[:, c : c + 1],
+            )
+            neg = sb.tile([P, 1], F32, name="neg_max%d" % c)
+            nc.scalar.activation(neg[:], chunk_max[:, c : c + 1], ACT.Copy, scale=-1.0)
+            p_chunk = sb.tile([P, CHUNK], F32, name="probs%d" % c)
+            nc.scalar.activation(p_chunk[:], scores[:, cols], ACT.Exp, bias=neg[:], accum_out=chunk_sum[:, c : c + 1])
+            probs.append(p_chunk)
+
+        neg_row_max = sb.tile([P, 1], F32, name="neg_row_max")
+        nc.vector.tensor_reduce(neg_row_max[:], chunk_max[:], mybir.AxisListType.X, ALU.max, negate=True)
+        rescale = sb.tile([P, CHUNKS], F32, name="rescale")
+        nc.scalar.activation(rescale[:], chunk_max[:], ACT.Exp, bias=neg_row_max[:])
+
+        logit = sb.tile([P, LISTED], F32, name="logit")
+        nc.vector.tensor_tensor(logit[:], scores[:].indirect(offsets[:]), lpo_sb[:], ALU.subtract)
+        ratio = sb.tile([P, LISTED], F32, name="ratio")
+        nc.scalar.activation(ratio[:], logit[:], ACT.Exp, bias=neg_row_max[:])
+
+        z_parts = sb.tile([P, CHUNKS], F32, name="z_parts")
+        z = sb.tile([P, 1], F32, name="z")
+        nc.vector.scalar_tensor_tensor(z_parts[:], chunk_sum[:], 1.0, rescale[:], ALU.mult, ALU.mult, accum_out=z[:])
+        z_inv = sb.tile([P, 1], F32, name="z_inv")
+        nc.vector.reciprocal(z_inv[:], z[:])
+        coef = sb.tile([P, CHUNKS], F32, name="coef")
+        nc.vector.tensor_scalar(out=coef[:], in0=rescale[:], scalar1=z_inv[:], scalar2=-1.0, op0=ALU.mult, op1=ALU.mult)
+
+        e1 = sb.tile([P, LISTED], F32, name="e1")
+        e1_sum = sb.tile([P, 1], F32, name="e1_sum")
+        nc.vector.scalar_tensor_tensor(e1[:], ratio[:], z_inv[:], adv_sb[:], ALU.mult, ALU.mult, accum_out=e1_sum[:])
+        nc.vector.tensor_copy(placed[:].indirect(offsets[:]), e1[:])
+
+        dz = sb.tile([P, CHUNKS], F32, name="dz")
+        nc.scalar.activation(dz[:], coef[:], ACT.Copy, scale=e1_sum[:])
+
+        blocks = [slice(b * P, (b + 1) * P) for b in range(BLOCKS)]
+        turned = []
+        for c in range(CHUNKS - 1):
+            bank = ps_col.tile([P, CHUNK], F32, name="turned", tag="col")
+            for b, blk in enumerate(blocks):
+                nc.tensor.matmul(bank[:, blk], old_sb[c][:, blk], ident[:], start=(b == 0), stop=False, is_transpose=True)
+            turned.append(bank)
+
+        def scale_and_turn(c):
+            scaled = ring.tile([P, CHUNK], F32, name="scaled")
+            nc.scalar.activation(scaled[:], probs[c][:], ACT.Copy, scale=dz[:, c : c + 1])
+            for b, blk in enumerate(blocks):
+                nc.tensor.matmul(turned[c][:, blk], scaled[:, blk], ident[:], start=False, stop=(b == BLOCKS - 1), is_transpose=True)
+
+        def turn_back(c):
+            turned_sb = sb.tile([P, CHUNK], F32, name="turned_sb%d" % c)
+            nc.scalar.copy(turned_sb[:], turned[c][:])
+            dense = ps_row.tile([P, CHUNK], F32, name="dense", tag="row")
+            for blk in blocks:
+                nc.tensor.transpose(dense[:, blk], turned_sb[:, blk], ident[:])
+            return dense
+
+        def finish(c, dense):
+            cols = slice(c * CHUNK, (c + 1) * CHUNK)
+            result = sb.tile([P, CHUNK], F32, name="result%d" % c)
+            nc.vector.tensor_tensor(result[:], dense[:], placed[:, cols], ALU.add)
+            nc.sync.dma_start(out=out[:, cols], in_=result[:])
+
+        last = CHUNKS - 1
+        scaled_last = sb.tile([P, CHUNK], F32, name="scaled_last")
+        nc.gpsimd.tensor_scalar(out=scaled_last[:], in0=probs[last][:], scalar1=dz[:, last : last + 1], scalar2=0.0, op0=ALU.mult, op1=ALU.add)
+        dense_last = sb.tile([P, CHUNK], F32, name="dense_last")
+        nc.gpsimd.tensor_tensor(dense_last[:], scaled_last[:], old_sb[last][:], ALU.add)
+
+        scale_and_turn(0)
+        scale_and_turn(1)
+        dense0 = turn_back(0)
+        scale_and_turn(2)
+        dense1 = turn_back(1)
+        dense2 = turn_back(2)
+        finish(0, dense0)
+        finish(1, dense1)
+        finish(last, dense_last)
+        finish(2, dense2)

@@ -22,16 +22,16 @@ PACK = 4
 CHUNK = 512
 CHUNKS = V // CHUNK
 HALF = V // 2
-BLOCKS = CHUNK // P
+SPLIT = 1280
+TURNED = [(lo, min(lo + CHUNK, SPLIT)) for lo in range(0, SPLIT, CHUNK)]
 
 
 def tile_attend_bpolicyratio_heads_kernel(tc, hid, voc_words, voc_scales, lpo, adv, old, offs, out):
     nc = tc.nc
     with ExitStack() as ctx:
         sb = ctx.enter_context(tc.tile_pool(name="sb", bufs=1))
-        ring = ctx.enter_context(tc.tile_pool(name="ring", bufs=2))
         ps_row = ctx.enter_context(tc.psum_pool(name="ps_row", bufs=CHUNKS))
-        ps_col = ctx.enter_context(tc.psum_pool(name="ps_col", bufs=CHUNKS - 1))
+        ps_col = ctx.enter_context(tc.psum_pool(name="ps_col", bufs=len(TURNED)))
 
         offsets = sb.tile([P, LISTED // 16], U16, name="offsets")
         voc_plane = sb.tile([P, V], U8, name="voc_plane", align_bytes=64)
@@ -58,11 +58,10 @@ def tile_attend_bpolicyratio_heads_kernel(tc, hid, voc_words, voc_scales, lpo, a
         nc.sync.dma_start(out=lpo_sb[:], in_=lpo)
         adv_sb = sb.tile([P, LISTED], F32, name="adv_sb")
         nc.sync.dma_start(out=adv_sb[:], in_=adv)
-        old_sb = []
-        for c in range(CHUNKS):
-            o = sb.tile([P, CHUNK], F32, name="old%d" % c)
-            nc.sync.dma_start(out=o[:], in_=old[:, c * CHUNK : (c + 1) * CHUNK])
-            old_sb.append(o)
+        old_sb = {}
+        for lo, hi in TURNED + [(SPLIT, V)]:
+            old_sb[lo] = sb.tile([P, hi - lo], F32, name="old%d" % lo)
+            nc.sync.dma_start(out=old_sb[lo][:], in_=old[:, lo:hi])
 
         placed = sb.tile([P, V], F32, name="placed")
         nc.vector.memset(placed[:], 0.0)
@@ -70,19 +69,26 @@ def tile_attend_bpolicyratio_heads_kernel(tc, hid, voc_words, voc_scales, lpo, a
         make_identity(nc, ident[:])
 
         hid_bf = sb.tile([P, Q, PACK], BF16, name="hid_bf", align_bytes=64)
-        nc.vector.tensor_copy(
-            out=hid_bf[:].rearrange("p (c i) t -> p c t i", i=4),
-            in_=hid_raw[:].rearrange("p t (c i) -> p c t i", i=4),
-        )
         hid_codes = sb.tile([P, Q], U32, name="hid_codes", align_bytes=64)
         hid_plane = sb.tile([P, Q], U8, name="hid_plane", align_bytes=64)
-        nc.vector.quantize_mx(out=hid_codes[:].bitcast(FP8X4), scales=hid_plane[:], in_=hid_bf[:].rearrange("p q t -> p (q t)"))
+        row_halves = [slice(0, Q // 2), slice(Q // 2, Q)]
+        for rows in row_halves:
+            nc.vector.tensor_copy(
+                out=hid_bf[:, rows, :].rearrange("p (c i) t -> p c t i", i=4),
+                in_=hid_raw[:, :, rows].rearrange("p t (c i) -> p c t i", i=4),
+            )
+        for rows in row_halves:
+            nc.vector.quantize_mx(
+                out=hid_codes[:, rows].bitcast(FP8X4), scales=hid_plane[:, rows], in_=hid_bf[:, rows, :].rearrange("p q t -> p (q t)")
+            )
 
         scores = sb.tile([P, V], F32, name="scores")
         chunk_max = sb.tile([P, CHUNKS], F32, name="chunk_max")
-        chunk_sum = sb.tile([P, CHUNKS], F32, name="chunk_sum")
-        probs = []
-        for c in range(CHUNKS):
+        neg_max = sb.tile([P, 2], F32, name="neg_max")
+        half_sum = sb.tile([P, 2], F32, name="half_sum")
+        probs = sb.tile([P, V], F32, name="probs")
+
+        def score(c):
             cols = slice(c * CHUNK, (c + 1) * CHUNK)
             bank = ps_row.tile([P, CHUNK], F32, name="bank", tag="row")
             nc.tensor.matmul_mx(
@@ -98,79 +104,81 @@ def tile_attend_bpolicyratio_heads_kernel(tc, hid, voc_words, voc_scales, lpo, a
                 out=scores[:, cols], in0=bank[:], scalar1=1.0, scalar2=None,
                 op0=ALU.mult, op1=ALU.max, accum_out=chunk_max[:, c : c + 1],
             )
-            neg = sb.tile([P, 1], F32, name="neg_max%d" % c)
-            nc.scalar.activation(neg[:], chunk_max[:, c : c + 1], ACT.Copy, scale=-1.0)
-            p_chunk = sb.tile([P, CHUNK], F32, name="probs%d" % c)
-            nc.scalar.activation(p_chunk[:], scores[:, cols], ACT.Exp, bias=neg[:], accum_out=chunk_sum[:, c : c + 1])
-            probs.append(p_chunk)
 
-        neg_row_max = sb.tile([P, 1], F32, name="neg_row_max")
-        nc.vector.tensor_reduce(neg_row_max[:], chunk_max[:], mybir.AxisListType.X, ALU.max, negate=True)
-        rescale = sb.tile([P, CHUNKS], F32, name="rescale")
-        nc.scalar.activation(rescale[:], chunk_max[:], ACT.Exp, bias=neg_row_max[:])
+        def exponentiate(half):
+            cols = slice(half * HALF, (half + 1) * HALF)
+            shift = neg_max[:, half : half + 1]
+            nc.vector.tensor_reduce(shift, chunk_max[:, : 2 * (half + 1)], mybir.AxisListType.X, ALU.max, negate=True)
+            nc.scalar.activation(probs[:, cols], scores[:, cols], ACT.Exp, bias=shift, accum_out=half_sum[:, half : half + 1])
+
+        score(0)
+        score(1)
+        score(2)
+        exponentiate(0)
+        score(3)
+        exponentiate(1)
+        neg_row_max = neg_max[:, 1:2]
+        rescale = sb.tile([P, 2], F32, name="rescale")
+        nc.scalar.activation(rescale[:], neg_max[:], ACT.Exp, bias=neg_row_max, scale=-1.0)
 
         logit = sb.tile([P, LISTED], F32, name="logit")
         nc.vector.tensor_tensor(logit[:], scores[:].indirect(offsets[:]), lpo_sb[:], ALU.subtract)
         ratio = sb.tile([P, LISTED], F32, name="ratio")
-        nc.scalar.activation(ratio[:], logit[:], ACT.Exp, bias=neg_row_max[:])
+        list_halves = [slice(0, LISTED // 2), slice(LISTED // 2, LISTED)]
+        for part in list_halves:
+            nc.scalar.activation(ratio[:, part], logit[:, part], ACT.Exp, bias=neg_row_max)
 
-        z_parts = sb.tile([P, CHUNKS], F32, name="z_parts")
         z = sb.tile([P, 1], F32, name="z")
-        nc.vector.scalar_tensor_tensor(z_parts[:], chunk_sum[:], 1.0, rescale[:], ALU.mult, ALU.mult, accum_out=z[:])
+        nc.vector.scalar_tensor_tensor(z[:], half_sum[:, 0:1], rescale[:, 0:1], half_sum[:, 1:2], ALU.mult, ALU.add)
         z_inv = sb.tile([P, 1], F32, name="z_inv")
         nc.vector.reciprocal(z_inv[:], z[:])
-        coef = sb.tile([P, CHUNKS], F32, name="coef")
+        coef = sb.tile([P, 2], F32, name="coef")
         nc.vector.tensor_scalar(out=coef[:], in0=rescale[:], scalar1=z_inv[:], scalar2=-1.0, op0=ALU.mult, op1=ALU.mult)
 
         e1 = sb.tile([P, LISTED], F32, name="e1")
-        e1_sum = sb.tile([P, 1], F32, name="e1_sum")
-        nc.vector.scalar_tensor_tensor(e1[:], ratio[:], z_inv[:], adv_sb[:], ALU.mult, ALU.mult, accum_out=e1_sum[:])
+        e1_sum = sb.tile([P, 2], F32, name="e1_sum")
+        for j, part in enumerate(list_halves):
+            nc.vector.scalar_tensor_tensor(
+                e1[:, part], ratio[:, part], z_inv[:], adv_sb[:, part], ALU.mult, ALU.mult, accum_out=e1_sum[:, j : j + 1]
+            )
+        dz = sb.tile([P, 2], F32, name="dz")
+        nc.vector.scalar_tensor_tensor(dz[:], e1_sum[:, 0:1].to_broadcast([P, 2]), e1_sum[:, 1:2], coef[:], ALU.add, ALU.mult)
         nc.vector.tensor_copy(placed[:].indirect(offsets[:]), e1[:])
 
-        dz = sb.tile([P, CHUNKS], F32, name="dz")
-        nc.scalar.activation(dz[:], coef[:], ACT.Copy, scale=e1_sum[:])
+        def blocks(lo, hi):
+            return [slice(b, b + P) for b in range(0, hi - lo, P)]
 
-        blocks = [slice(b * P, (b + 1) * P) for b in range(BLOCKS)]
-        turned = []
-        for c in range(CHUNKS - 1):
-            bank = ps_col.tile([P, CHUNK], F32, name="turned", tag="col")
-            for b, blk in enumerate(blocks):
-                nc.tensor.matmul(bank[:, blk], old_sb[c][:, blk], ident[:], start=(b == 0), stop=False, is_transpose=True)
-            turned.append(bank)
+        turned = {}
+        for lo, hi in TURNED:
+            turned[lo] = ps_col.tile([P, hi - lo], F32, name="turned", tag="col")
+            for blk in blocks(lo, hi):
+                nc.tensor.matmul(turned[lo][:, blk], old_sb[lo][:, blk], ident[:], start=(blk.start == 0), stop=False, is_transpose=True)
 
-        def scale_and_turn(c):
-            scaled = ring.tile([P, CHUNK], F32, name="scaled")
-            nc.scalar.activation(scaled[:], probs[c][:], ACT.Copy, scale=dz[:, c : c + 1])
-            for b, blk in enumerate(blocks):
-                nc.tensor.matmul(turned[c][:, blk], scaled[:, blk], ident[:], start=False, stop=(b == BLOCKS - 1), is_transpose=True)
+        scaled_rest = sb.tile([P, V - SPLIT], F32, name="scaled_rest")
+        nc.gpsimd.tensor_scalar(out=scaled_rest[:], in0=probs[:, SPLIT:], scalar1=dz[:, 1:2], scalar2=0.0, op0=ALU.mult, op1=ALU.add)
+        dense_rest = sb.tile([P, V - SPLIT], F32, name="dense_rest")
+        nc.gpsimd.tensor_tensor(dense_rest[:], scaled_rest[:], old_sb[SPLIT][:], ALU.add)
 
-        def turn_back(c):
-            turned_sb = sb.tile([P, CHUNK], F32, name="turned_sb%d" % c)
-            nc.scalar.copy(turned_sb[:], turned[c][:])
-            dense = ps_row.tile([P, CHUNK], F32, name="dense", tag="row")
-            for blk in blocks:
-                nc.tensor.transpose(dense[:, blk], turned_sb[:, blk], ident[:])
-            return dense
+        for lo, hi in TURNED:
+            scaled = sb.tile([P, hi - lo], F32, name="scaled%d" % lo)
+            nc.scalar.activation(scaled[:], probs[:, lo:hi], ACT.Copy, scale=dz[:, lo // HALF : lo // HALF + 1])
+            for blk in blocks(lo, hi):
+                nc.tensor.matmul(turned[lo][:, blk], scaled[:, blk], ident[:], start=False, stop=(blk.stop == hi - lo), is_transpose=True)
 
-        def finish(c, dense):
-            cols = slice(c * CHUNK, (c + 1) * CHUNK)
-            result = sb.tile([P, CHUNK], F32, name="result%d" % c)
-            nc.vector.tensor_tensor(result[:], dense[:], placed[:, cols], ALU.add)
-            nc.sync.dma_start(out=out[:, cols], in_=result[:])
+        dense = {}
+        for lo, hi in TURNED:
+            turned_sb = sb.tile([P, hi - lo], F32, name="turned_sb%d" % lo)
+            nc.scalar.copy(turned_sb[:], turned[lo][:])
+            dense[lo] = ps_row.tile([P, hi - lo], F32, name="dense", tag="row")
+            for blk in blocks(lo, hi):
+                nc.tensor.transpose(dense[lo][:, blk], turned_sb[:, blk], ident[:])
 
-        last = CHUNKS - 1
-        scaled_last = sb.tile([P, CHUNK], F32, name="scaled_last")
-        nc.gpsimd.tensor_scalar(out=scaled_last[:], in0=probs[last][:], scalar1=dz[:, last : last + 1], scalar2=0.0, op0=ALU.mult, op1=ALU.add)
-        dense_last = sb.tile([P, CHUNK], F32, name="dense_last")
-        nc.gpsimd.tensor_tensor(dense_last[:], scaled_last[:], old_sb[last][:], ALU.add)
+        def finish(lo, hi, dense_part):
+            result = sb.tile([P, hi - lo], F32, name="result%d" % lo)
+            nc.vector.tensor_tensor(result[:], dense_part, placed[:, lo:hi], ALU.add)
+            nc.sync.dma_start(out=out[:, lo:hi], in_=result[:])
 
-        scale_and_turn(0)
-        scale_and_turn(1)
-        dense0 = turn_back(0)
-        scale_and_turn(2)
-        dense1 = turn_back(1)
-        dense2 = turn_back(2)
-        finish(0, dense0)
-        finish(1, dense1)
-        finish(last, dense_last)
-        finish(2, dense2)
+        finish(SPLIT, SPLIT + 256, dense_rest[:, :256])
+        finish(SPLIT + 256, V, dense_rest[:, 256:])
+        for lo, hi in TURNED:
+            finish(lo, hi, dense[lo][:])

@@ -23,7 +23,7 @@ CHUNK = 512
 CHUNKS = V // CHUNK
 HALF = V // 2
 SPLIT = 1280
-TURNED = [(lo, min(lo + CHUNK, SPLIT)) for lo in range(0, SPLIT, CHUNK)]
+TURNED = [(0, CHUNK), (CHUNK, HALF), (HALF, SPLIT)]
 
 
 def tile_attend_bpolicyratio_heads_kernel(tc, hid, voc_words, voc_scales, lpo, adv, old, offs, out):
@@ -36,23 +36,30 @@ def tile_attend_bpolicyratio_heads_kernel(tc, hid, voc_words, voc_scales, lpo, a
         offsets = sb.tile([P, LISTED // 16], U16, name="offsets")
         voc_plane = sb.tile([P, V], U8, name="voc_plane", align_bytes=64)
         nc.vector.memset(voc_plane[:].bitcast(I32), 0)
-        warm_in = sb.tile([P, 1], F32, name="warm_in")
-        nc.gpsimd.memset(warm_in[:], 0.0)
-        warm_out = sb.tile([P, 1], F32, name="warm_out")
-        nc.scalar.activation(warm_out[:], warm_in[:], ACT.Exp)
+
+        zero = sb.tile([P, 1], F32, name="zero")
+        nc.gpsimd.memset(zero[:], 0.0)
+        rescale = sb.tile([P, 3], F32, name="rescale")
+        nc.scalar.activation(rescale[:, 2:3], zero[:], ACT.Exp)
 
         hid_raw = sb.tile([P, PACK, Q], F32, name="hid_raw")
         nc.sync.dma_start(out=hid_raw[:], in_=hid.rearrange("(p t) q -> p t q", t=PACK))
+        words = {}
+
+        def load_words(lo, hi):
+            w = sb.tile([P, 2 * (hi - lo)], U8, name="words%d" % lo, align_bytes=64)
+            nc.sync.dma_start(out=w[:].bitcast(I32), in_=voc_words[0, :, 2 * lo : 2 * hi].bitcast(I32))
+            for col in range(lo, hi, CHUNK):
+                words[col // CHUNK] = w[:, 2 * (col - lo) : 2 * (col - lo + CHUNK)]
+
+        load_words(0, CHUNK)
         for quad in range(4):
             nc.sync.dma_start(
                 out=voc_plane[32 * quad : 32 * quad + 4, :].bitcast(I32),
                 in_=voc_scales[0, 4 * quad : 4 * quad + 4, :].bitcast(I32),
             )
-        words = []
-        for half in range(2):
-            w = sb.tile([P, 2 * HALF], U8, name="words%d" % half, align_bytes=64)
-            nc.sync.dma_start(out=w[:].bitcast(I32), in_=voc_words[0, :, half * 2 * HALF : (half + 1) * 2 * HALF].bitcast(I32))
-            words.append(w)
+        load_words(CHUNK, HALF)
+        load_words(HALF, V)
         nc.sync.dma_start(offsets[:], offs)
         lpo_sb = sb.tile([P, LISTED], F32, name="lpo_sb")
         nc.sync.dma_start(out=lpo_sb[:], in_=lpo)
@@ -84,8 +91,9 @@ def tile_attend_bpolicyratio_heads_kernel(tc, hid, voc_words, voc_scales, lpo, a
 
         scores = sb.tile([P, V], F32, name="scores")
         chunk_max = sb.tile([P, CHUNKS], F32, name="chunk_max")
-        neg_max = sb.tile([P, 2], F32, name="neg_max")
-        half_sum = sb.tile([P, 2], F32, name="half_sum")
+        neg_early = sb.tile([P, 2], F32, name="neg_early")
+        neg_row_max = sb.tile([P, 1], F32, name="neg_row_max")
+        part_sum = sb.tile([P, 3], F32, name="part_sum")
         probs = sb.tile([P, V], F32, name="probs")
 
         def score(c):
@@ -95,7 +103,7 @@ def tile_attend_bpolicyratio_heads_kernel(tc, hid, voc_words, voc_scales, lpo, a
                 out=bank[:],
                 lhsT=hid_codes[:].bitcast(FP8X4),
                 lhsT_scale=hid_plane[:],
-                rhs=words[c // 2][:, (c % 2) * 2 * CHUNK : (c % 2 + 1) * 2 * CHUNK].bitcast(FP4X4),
+                rhs=words[c].bitcast(FP4X4),
                 rhs_scale=voc_plane[:, cols],
                 start=True,
                 stop=True,
@@ -105,34 +113,33 @@ def tile_attend_bpolicyratio_heads_kernel(tc, hid, voc_words, voc_scales, lpo, a
                 op0=ALU.mult, op1=ALU.max, accum_out=chunk_max[:, c : c + 1],
             )
 
-        def exponentiate(half):
-            cols = slice(half * HALF, (half + 1) * HALF)
-            shift = neg_max[:, half : half + 1]
-            nc.vector.tensor_reduce(shift, chunk_max[:, : 2 * (half + 1)], mybir.AxisListType.X, ALU.max, negate=True)
-            nc.scalar.activation(probs[:, cols], scores[:, cols], ACT.Exp, bias=shift, accum_out=half_sum[:, half : half + 1])
+        def exponentiate(part, lo, hi, neg_shift):
+            nc.scalar.activation(probs[:, lo:hi], scores[:, lo:hi], ACT.Exp, bias=neg_shift, accum_out=part_sum[:, part : part + 1])
 
         score(0)
         score(1)
+        nc.scalar.activation(neg_early[:], chunk_max[:, 0:2], ACT.Copy, scale=-1.0)
+        exponentiate(0, 0, CHUNK, neg_early[:, 0:1])
+        exponentiate(1, CHUNK, HALF, neg_early[:, 1:2])
         score(2)
-        exponentiate(0)
         score(3)
-        exponentiate(1)
-        neg_row_max = neg_max[:, 1:2]
-        rescale = sb.tile([P, 2], F32, name="rescale")
-        nc.scalar.activation(rescale[:], neg_max[:], ACT.Exp, bias=neg_row_max, scale=-1.0)
+        nc.vector.tensor_reduce(neg_row_max[:], chunk_max[:], mybir.AxisListType.X, ALU.max, negate=True)
+        nc.scalar.activation(rescale[:, 0:2], chunk_max[:, 0:2], ACT.Exp, bias=neg_row_max[:])
+        exponentiate(2, HALF, V, neg_row_max[:])
 
         logit = sb.tile([P, LISTED], F32, name="logit")
         nc.vector.tensor_tensor(logit[:], scores[:].indirect(offsets[:]), lpo_sb[:], ALU.subtract)
         ratio = sb.tile([P, LISTED], F32, name="ratio")
         list_halves = [slice(0, LISTED // 2), slice(LISTED // 2, LISTED)]
         for part in list_halves:
-            nc.scalar.activation(ratio[:, part], logit[:, part], ACT.Exp, bias=neg_row_max)
+            nc.scalar.activation(ratio[:, part], logit[:, part], ACT.Exp, bias=neg_row_max[:])
 
         z = sb.tile([P, 1], F32, name="z")
-        nc.vector.scalar_tensor_tensor(z[:], half_sum[:, 0:1], rescale[:, 0:1], half_sum[:, 1:2], ALU.mult, ALU.add)
+        z_parts = sb.tile([P, 3], F32, name="z_parts")
+        nc.vector.scalar_tensor_tensor(z_parts[:], part_sum[:], 1.0, rescale[:], ALU.mult, ALU.mult, accum_out=z[:])
         z_inv = sb.tile([P, 1], F32, name="z_inv")
         nc.vector.reciprocal(z_inv[:], z[:])
-        coef = sb.tile([P, 2], F32, name="coef")
+        coef = sb.tile([P, 3], F32, name="coef")
         nc.vector.tensor_scalar(out=coef[:], in0=rescale[:], scalar1=z_inv[:], scalar2=-1.0, op0=ALU.mult, op1=ALU.mult)
 
         e1 = sb.tile([P, LISTED], F32, name="e1")
@@ -141,8 +148,8 @@ def tile_attend_bpolicyratio_heads_kernel(tc, hid, voc_words, voc_scales, lpo, a
             nc.vector.scalar_tensor_tensor(
                 e1[:, part], ratio[:, part], z_inv[:], adv_sb[:, part], ALU.mult, ALU.mult, accum_out=e1_sum[:, j : j + 1]
             )
-        dz = sb.tile([P, 2], F32, name="dz")
-        nc.vector.scalar_tensor_tensor(dz[:], e1_sum[:, 0:1].to_broadcast([P, 2]), e1_sum[:, 1:2], coef[:], ALU.add, ALU.mult)
+        dz = sb.tile([P, 3], F32, name="dz")
+        nc.vector.scalar_tensor_tensor(dz[:], e1_sum[:, 0:1].to_broadcast([P, 3]), e1_sum[:, 1:2], coef[:], ALU.add, ALU.mult)
         nc.vector.tensor_copy(placed[:].indirect(offsets[:]), e1[:])
 
         def blocks(lo, hi):
@@ -150,18 +157,18 @@ def tile_attend_bpolicyratio_heads_kernel(tc, hid, voc_words, voc_scales, lpo, a
 
         turned = {}
         for lo, hi in TURNED:
-            turned[lo] = ps_col.tile([P, hi - lo], F32, name="turned", tag="col")
+            turned[lo] = ps_row.tile([P, hi - lo], F32, name="turned", tag="row")
             for blk in blocks(lo, hi):
                 nc.tensor.matmul(turned[lo][:, blk], old_sb[lo][:, blk], ident[:], start=(blk.start == 0), stop=False, is_transpose=True)
 
         scaled_rest = sb.tile([P, V - SPLIT], F32, name="scaled_rest")
-        nc.gpsimd.tensor_scalar(out=scaled_rest[:], in0=probs[:, SPLIT:], scalar1=dz[:, 1:2], scalar2=0.0, op0=ALU.mult, op1=ALU.add)
+        nc.gpsimd.tensor_scalar(out=scaled_rest[:], in0=probs[:, SPLIT:], scalar1=dz[:, 2:3], scalar2=0.0, op0=ALU.mult, op1=ALU.add)
         dense_rest = sb.tile([P, V - SPLIT], F32, name="dense_rest")
         nc.gpsimd.tensor_tensor(dense_rest[:], scaled_rest[:], old_sb[SPLIT][:], ALU.add)
 
         for lo, hi in TURNED:
             scaled = sb.tile([P, hi - lo], F32, name="scaled%d" % lo)
-            nc.scalar.activation(scaled[:], probs[:, lo:hi], ACT.Copy, scale=dz[:, lo // HALF : lo // HALF + 1])
+            nc.scalar.activation(scaled[:], probs[:, lo:hi], ACT.Copy, scale=dz[:, lo // CHUNK : lo // CHUNK + 1])
             for blk in blocks(lo, hi):
                 nc.tensor.matmul(turned[lo][:, blk], scaled[:, blk], ident[:], start=False, stop=(blk.stop == hi - lo), is_transpose=True)
 
@@ -169,7 +176,7 @@ def tile_attend_bpolicyratio_heads_kernel(tc, hid, voc_words, voc_scales, lpo, a
         for lo, hi in TURNED:
             turned_sb = sb.tile([P, hi - lo], F32, name="turned_sb%d" % lo)
             nc.scalar.copy(turned_sb[:], turned[lo][:])
-            dense[lo] = ps_row.tile([P, hi - lo], F32, name="dense", tag="row")
+            dense[lo] = ps_col.tile([P, hi - lo], F32, name="dense", tag="col")
             for blk in blocks(lo, hi):
                 nc.tensor.transpose(dense[lo][:, blk], turned_sb[:, blk], ident[:])
 

@@ -22,6 +22,7 @@ PACK = 4
 CHUNK = 512
 CHUNKS = V // CHUNK
 HALF = V // 2
+STORE = 256
 SPLIT = 1280
 TURNED = [(0, CHUNK), (CHUNK, HALF), (HALF, SPLIT)]
 
@@ -181,11 +182,11 @@ def tile_attend_bpolicyratio_heads_kernel(tc, hid, voc_words, voc_scales, lpo, a
                 nc.tensor.transpose(dense[lo][:, blk], turned_sb[:, blk], ident[:])
 
         def finish(lo, hi, dense_part):
-            result = sb.tile([P, hi - lo], F32, name="result%d" % lo)
-            nc.vector.tensor_tensor(result[:], dense_part, placed[:, lo:hi], ALU.add)
-            nc.sync.dma_start(out=out[:, lo:hi], in_=result[:])
+            for start in range(lo, hi, STORE):
+                result = sb.tile([P, STORE], F32, name="result%d" % start)
+                nc.vector.tensor_tensor(result[:], dense_part[:, start - lo : start - lo + STORE], placed[:, start : start + STORE], ALU.add)
+                nc.sync.dma_start(out=out[:, start : start + STORE], in_=result[:])
 
-        finish(SPLIT, SPLIT + 256, dense_rest[:, :256])
-        finish(SPLIT + 256, V, dense_rest[:, 256:])
+        finish(SPLIT, V, dense_rest)
         for lo, hi in TURNED:
-            finish(lo, hi, dense[lo][:])
+            finish(lo, hi, dense[lo])

from contextlib import ExitStack

import concourse.mybir as mybir
from concourse.masks import make_identity

D, V, Q, LISTED = 512, 2048, 128, 512
FLOPS = 2 * D * V * Q

F32 = mybir.dt.float32
BF16 = mybir.dt.bfloat16
I32 = mybir.dt.int32
U32 = mybir.dt.uint32
U16 = mybir.dt.uint16
U8 = mybir.dt.uint8
FP8X4 = mybir.dt.float8_e4m3fn_x4
FP4X4 = mybir.dt.float4_e2m1fn_x4
ALU = mybir.AluOpType
ACT = mybir.ActivationFunctionType

P = 128
PACK = 4
CHUNK = 512
CHUNKS = V // CHUNK
HALF = V // 2
STORE = 256
SPLIT = 1280
TURNED = [(0, CHUNK), (CHUNK, HALF), (HALF, SPLIT)]


def tile_attend_bpolicyratio_heads_kernel(tc, hid, voc_words, voc_scales, lpo, adv, old, offs, out):
    nc = tc.nc
    with ExitStack() as ctx:
        sb = ctx.enter_context(tc.tile_pool(name="sb", bufs=1))
        ps_row = ctx.enter_context(tc.psum_pool(name="ps_row", bufs=CHUNKS))
        ps_col = ctx.enter_context(tc.psum_pool(name="ps_col", bufs=len(TURNED)))

        offsets = sb.tile([P, LISTED // 16], U16, name="offsets")
        voc_plane = sb.tile([P, V], U8, name="voc_plane", align_bytes=64)
        nc.vector.memset(voc_plane[:].bitcast(I32), 0)

        zero = sb.tile([P, 1], F32, name="zero")
        nc.gpsimd.memset(zero[:], 0.0)
        rescale = sb.tile([P, 3], F32, name="rescale")
        nc.scalar.activation(rescale[:, 2:3], zero[:], ACT.Exp)

        hid_raw = sb.tile([P, PACK, Q], F32, name="hid_raw")
        nc.sync.dma_start(out=hid_raw[:], in_=hid.rearrange("(p t) q -> p t q", t=PACK))
        words = {}

        def load_words(lo, hi):
            w = sb.tile([P, 2 * (hi - lo)], U8, name="words%d" % lo, align_bytes=64)
            nc.sync.dma_start(out=w[:].bitcast(I32), in_=voc_words[0, :, 2 * lo : 2 * hi].bitcast(I32))
            for col in range(lo, hi, CHUNK):
                words[col // CHUNK] = w[:, 2 * (col - lo) : 2 * (col - lo + CHUNK)]

        load_words(0, CHUNK)
        for quad in range(4):
            nc.sync.dma_start(
                out=voc_plane[32 * quad : 32 * quad + 4, :].bitcast(I32),
                in_=voc_scales[0, 4 * quad : 4 * quad + 4, :].bitcast(I32),
            )
        load_words(CHUNK, HALF)
        load_words(HALF, V)
        nc.sync.dma_start(offsets[:], offs)
        lpo_sb = sb.tile([P, LISTED], F32, name="lpo_sb")
        nc.sync.dma_start(out=lpo_sb[:], in_=lpo)
        adv_sb = sb.tile([P, LISTED], F32, name="adv_sb")
        nc.sync.dma_start(out=adv_sb[:], in_=adv)
        old_sb = {}
        for lo, hi in TURNED + [(SPLIT, V)]:
            old_sb[lo] = sb.tile([P, hi - lo], F32, name="old%d" % lo)
            nc.sync.dma_start(out=old_sb[lo][:], in_=old[:, lo:hi])

        placed = sb.tile([P, V], F32, name="placed")
        nc.vector.memset(placed[:], 0.0)
        ident = sb.tile([P, P], F32, name="ident")
        make_identity(nc, ident[:])

        hid_bf = sb.tile([P, Q, PACK], BF16, name="hid_bf", align_bytes=64)
        hid_codes = sb.tile([P, Q], U32, name="hid_codes", align_bytes=64)
        hid_plane = sb.tile([P, Q], U8, name="hid_plane", align_bytes=64)
        row_halves = [slice(0, Q // 2), slice(Q // 2, Q)]
        for rows in row_halves:
            nc.vector.tensor_copy(
                out=hid_bf[:, rows, :].rearrange("p (c i) t -> p c t i", i=4),
                in_=hid_raw[:, :, rows].rearrange("p t (c i) -> p c t i", i=4),
            )
        for rows in row_halves:
            nc.vector.quantize_mx(
                out=hid_codes[:, rows].bitcast(FP8X4), scales=hid_plane[:, rows], in_=hid_bf[:, rows, :].rearrange("p q t -> p (q t)")
            )

        scores = sb.tile([P, V], F32, name="scores")
        chunk_max = sb.tile([P, CHUNKS], F32, name="chunk_max")
        neg_early = sb.tile([P, 2], F32, name="neg_early")
        neg_row_max = sb.tile([P, 1], F32, name="neg_row_max")
        part_sum = sb.tile([P, 3], F32, name="part_sum")
        probs = sb.tile([P, V], F32, name="probs")

        def score(c):
            cols = slice(c * CHUNK, (c + 1) * CHUNK)
            bank = ps_row.tile([P, CHUNK], F32, name="bank", tag="row")
            nc.tensor.matmul_mx(
                out=bank[:],
                lhsT=hid_codes[:].bitcast(FP8X4),
                lhsT_scale=hid_plane[:],
                rhs=words[c].bitcast(FP4X4),
                rhs_scale=voc_plane[:, cols],
                start=True,
                stop=True,
            )
            nc.vector.tensor_scalar(
                out=scores[:, cols], in0=bank[:], scalar1=1.0, scalar2=None,
                op0=ALU.mult, op1=ALU.max, accum_out=chunk_max[:, c : c + 1],
            )

        def exponentiate(part, lo, hi, neg_shift):
            nc.scalar.activation(probs[:, lo:hi], scores[:, lo:hi], ACT.Exp, bias=neg_shift, accum_out=part_sum[:, part : part + 1])

        score(0)
        score(1)
        nc.scalar.activation(neg_early[:], chunk_max[:, 0:2], ACT.Copy, scale=-1.0)
        exponentiate(0, 0, CHUNK, neg_early[:, 0:1])
        exponentiate(1, CHUNK, HALF, neg_early[:, 1:2])
        score(2)
        score(3)
        nc.vector.tensor_reduce(neg_row_max[:], chunk_max[:], mybir.AxisListType.X, ALU.max, negate=True)
        nc.scalar.activation(rescale[:, 0:2], chunk_max[:, 0:2], ACT.Exp, bias=neg_row_max[:])
        exponentiate(2, HALF, V, neg_row_max[:])

        logit = sb.tile([P, LISTED], F32, name="logit")
        nc.vector.tensor_tensor(logit[:], scores[:].indirect(offsets[:]), lpo_sb[:], ALU.subtract)
        ratio = sb.tile([P, LISTED], F32, name="ratio")
        list_halves = [slice(0, LISTED // 2), slice(LISTED // 2, LISTED)]
        for part in list_halves:
            nc.scalar.activation(ratio[:, part], logit[:, part], ACT.Exp, bias=neg_row_max[:])

        z = sb.tile([P, 1], F32, name="z")
        z_parts = sb.tile([P, 3], F32, name="z_parts")
        nc.vector.scalar_tensor_tensor(z_parts[:], part_sum[:], 1.0, rescale[:], ALU.mult, ALU.mult, accum_out=z[:])
        z_inv = sb.tile([P, 1], F32, name="z_inv")
        nc.vector.reciprocal(z_inv[:], z[:])
        coef = sb.tile([P, 3], F32, name="coef")
        nc.vector.tensor_scalar(out=coef[:], in0=rescale[:], scalar1=z_inv[:], scalar2=-1.0, op0=ALU.mult, op1=ALU.mult)

        e1 = sb.tile([P, LISTED], F32, name="e1")
        e1_sum = sb.tile([P, 2], F32, name="e1_sum")
        for j, part in enumerate(list_halves):
            nc.vector.scalar_tensor_tensor(
                e1[:, part], ratio[:, part], z_inv[:], adv_sb[:, part], ALU.mult, ALU.mult, accum_out=e1_sum[:, j : j + 1]
            )
        dz = sb.tile([P, 3], F32, name="dz")
        nc.vector.scalar_tensor_tensor(dz[:], e1_sum[:, 0:1].to_broadcast([P, 3]), e1_sum[:, 1:2], coef[:], ALU.add, ALU.mult)
        nc.vector.tensor_copy(placed[:].indirect(offsets[:]), e1[:])

        def blocks(lo, hi):
            return [slice(b, b + P) for b in range(0, hi - lo, P)]

        turned = {}
        for lo, hi in TURNED:
            turned[lo] = ps_row.tile([P, hi - lo], F32, name="turned", tag="row")
            for blk in blocks(lo, hi):
                nc.tensor.matmul(turned[lo][:, blk], old_sb[lo][:, blk], ident[:], start=(blk.start == 0), stop=False, is_transpose=True)

        scaled_rest = sb.tile([P, V - SPLIT], F32, name="scaled_rest")
        nc.gpsimd.tensor_scalar(out=scaled_rest[:], in0=probs[:, SPLIT:], scalar1=dz[:, 2:3], scalar2=0.0, op0=ALU.mult, op1=ALU.add)
        dense_rest = sb.tile([P, V - SPLIT], F32, name="dense_rest")
        nc.gpsimd.tensor_tensor(dense_rest[:], scaled_rest[:], old_sb[SPLIT][:], ALU.add)

        for lo, hi in TURNED:
            scaled = sb.tile([P, hi - lo], F32, name="scaled%d" % lo)
            nc.scalar.activation(scaled[:], probs[:, lo:hi], ACT.Copy, scale=dz[:, lo // CHUNK : lo // CHUNK + 1])
            for blk in blocks(lo, hi):
                nc.tensor.matmul(turned[lo][:, blk], scaled[:, blk], ident[:], start=False, stop=(blk.stop == hi - lo), is_transpose=True)

        dense = {}
        for lo, hi in TURNED:
            turned_sb = sb.tile([P, hi - lo], F32, name="turned_sb%d" % lo)
            nc.scalar.copy(turned_sb[:], turned[lo][:])
            dense[lo] = ps_col.tile([P, hi - lo], F32, name="dense", tag="col")
            for blk in blocks(lo, hi):
                nc.tensor.transpose(dense[lo][:, blk], turned_sb[:, blk], ident[:])

        def finish(lo, hi, dense_part):
            for start in range(lo, hi, STORE):
                result = sb.tile([P, STORE], F32, name="result%d" % start)
                nc.vector.tensor_tensor(result[:], dense_part[:, start - lo : start - lo + STORE], placed[:, start : start + STORE], ALU.add)
                nc.sync.dma_start(out=out[:, start : start + STORE], in_=result[:])

        finish(SPLIT, V, dense_rest)
        for lo, hi in TURNED:
            finish(lo, hi, dense[lo])
